import numpy as np
import ml_dtypes


def mxq(x, axis, fmt="e4m3"):
    dtype, down = {"e4m3": (ml_dtypes.float8_e4m3fn, 7), "e5m2": (ml_dtypes.float8_e5m2, 14)}[fmt]
    v = np.moveaxis(np.asarray(x, np.float32).astype(ml_dtypes.bfloat16).astype(np.float64), axis, -1)
    blocks = v.reshape(v.shape[:-1] + (-1, 32))
    amax = np.abs(blocks).max(-1, keepdims=True)
    byte = np.maximum(np.where(amax > 0, np.frexp(amax)[1] - 1 + 127, 0) - down, 1)
    scale = np.exp2(byte - 127.0)
    codes = (blocks / scale).astype(np.float32).astype(dtype).astype(np.float64)
    return np.moveaxis((codes * scale).reshape(v.shape), -1, axis)


WIDE = False


def mx_kscale(k):
    if not WIDE:
        return np.ones(k)
    levels = np.array([10, -10, 5, -5, 0])
    if k % 512:
        return np.exp2(np.random.permutation(np.resize(levels, k // 32))).repeat(32)
    a = np.empty((k // 512, 16))
    for p in range(k // 512):
        a[p, :8] = np.random.permutation(np.resize(levels, 8))
        for g in range(8):
            far = levels[np.abs(levels - a[p, g]) >= 10]
            a[p, g + 8] = far[np.random.randint(len(far))]
    return np.exp2(a.ravel()).repeat(32)


def f64(x):
    return np.asarray(x).astype(np.float64)


def striped(idx):
    return np.tile(idx.reshape(-1, 16).T, (8, 1)).astype(np.uint16)


def unstriped(offs):
    return offs[:16].T.reshape(-1).astype(np.int64)


E2M1 = np.array([0.0, 0.5, 1.0, 1.5, 2.0, 3.0, 4.0, 6.0, -0.0, -0.5, -1.0, -1.5, -2.0, -3.0, -4.0, -6.0])


def pack_weight(w, fmt):
    k, n = w.shape
    w = f64(np.asarray(w, np.float32).astype(ml_dtypes.bfloat16)).reshape(k // 32, 32, n)
    amax = np.abs(w).max(1)
    if fmt == "e4m3":
        byte = np.frexp(amax)[1] - 1 + 127 - 7
    else:
        mant, ex = np.frexp(amax / 6.0)
        byte = np.where(mant > 0.5, ex, ex - 1) + 127
    byte = np.clip(np.where(amax > 0, byte, 1), 1, 254)
    scaled = (w * np.exp2(127.0 - byte)[:, None, :]).reshape(k, n).astype(np.float32)
    by_word = np.ascontiguousarray(scaled.reshape(k // 512, 128, 4, n).transpose(0, 1, 3, 2))
    if fmt == "e4m3":
        words = by_word.astype(ml_dtypes.float8_e4m3fn).view(np.uint8)
    else:
        c = by_word.astype(ml_dtypes.float4_e2m1fn).view(np.uint8) & 0xF
        words = (c[..., 0::2] | (c[..., 1::2] << 4)).reshape(k // 512, 128, 2 * n)
    return np.ascontiguousarray(words), np.ascontiguousarray(byte.astype(np.uint8).reshape(k // 512, 16, n))


def unpack_weight(words, scales, fmt):
    g, _, n = scales.shape
    words = np.ascontiguousarray(words).reshape(g, 128, n, -1)
    if fmt == "e4m3":
        vals = words.view(ml_dtypes.float8_e4m3fn).astype(np.float64)
    else:
        nib = np.empty((g, 128, n, 4), np.uint8)
        nib[..., 0::2] = words & 0xF
        nib[..., 1::2] = words >> 4
        vals = E2M1[nib]
    vals = vals * np.repeat(np.exp2(scales.astype(np.float64) - 127.0), 8, axis=1)[..., None]
    return vals.transpose(0, 1, 3, 2).reshape(g * 512, n)


def planes(y):
    n, m = y.shape
    v = y.astype(np.float32).astype(ml_dtypes.bfloat16).astype(np.float64).reshape(n // 32, 32, m)
    top = np.abs(v).max(1)
    byte = np.clip(np.where(top > 0, np.frexp(top)[1] - 1 + 127 - 7, 1), 1, 254)
    codes = (v * np.exp2(127.0 - byte)[:, None, :]).reshape(n, m).astype(np.float32).astype(ml_dtypes.float8_e4m3fn).view(np.uint8)
    words = codes.reshape(n // 512, 128, 4, m).transpose(0, 1, 3, 2)
    return np.ascontiguousarray(words), np.ascontiguousarray(byte.astype(np.uint8).reshape(n // 512, 16, m))


def gelu(v):
    return 0.5 * v * (1.0 + np.tanh(np.sqrt(2.0 / np.pi) * (v + 0.044715 * v**3)))


K, T, E, C, H, N, HOT = 512, 512, 6, 256, 512, 512, 1


def by_expert(wq, xq):
    return np.concatenate([wq[e].T @ xq[:, e * C:(e + 1) * C] for e in range(E)], axis=1)


def setup_inputs():
    n = np.random.standard_normal
    s = mx_kscale(K)
    u = mx_kscale(H)
    slot_token = np.concatenate([np.random.permutation(T)[:C] for e in range(E)])
    x = pack_weight(n((K, T)) * s[:, None], "e4m3")
    w1h = [pack_weight(m, "e4m3") for m in n((HOT, K, H)) / np.sqrt(K) / s[None, :, None]]
    w3h = [pack_weight(m, "e4m3") for m in n((HOT, K, H)) / np.sqrt(K) / s[None, :, None] * u]
    w2h = [pack_weight(m, "e4m3") for m in n((HOT, H, N)) / np.sqrt(H) / u[None, :, None]]
    w1c = [pack_weight(m, "e2m1") for m in n((E - HOT, K, H)) / np.sqrt(K) / s[None, :, None]]
    w3c = [pack_weight(m, "e2m1") for m in n((E - HOT, K, H)) / np.sqrt(K) / s[None, :, None] * u]
    w2c = [pack_weight(m, "e2m1") for m in n((E - HOT, H, N)) / np.sqrt(H) / u[None, :, None]]
    return {
        "x_words": x[0],
        "x_scales": x[1],
        "w1h_words": np.stack([m[0] for m in w1h]),
        "w1h_scales": np.stack([m[1] for m in w1h]),
        "w3h_words": np.stack([m[0] for m in w3h]),
        "w3h_scales": np.stack([m[1] for m in w3h]),
        "w2h_words": np.stack([m[0] for m in w2h]),
        "w2h_scales": np.stack([m[1] for m in w2h]),
        "w1c_words": np.stack([m[0] for m in w1c]),
        "w1c_scales": np.stack([m[1] for m in w1c]),
        "w3c_words": np.stack([m[0] for m in w3c]),
        "w3c_scales": np.stack([m[1] for m in w3c]),
        "w2c_words": np.stack([m[0] for m in w2c]),
        "w2c_scales": np.stack([m[1] for m in w2c]),
        "offs": striped(slot_token),
    }


def reference(x_words, x_scales, w1h_words, w1h_scales, w3h_words, w3h_scales, w2h_words, w2h_scales, w1c_words, w1c_scales, w3c_words, w3c_scales, w2c_words, w2c_scales, offs):
    w1h = np.stack([unpack_weight(w1h_words[e], w1h_scales[e], "e4m3") for e in range(HOT)])
    w3h = np.stack([unpack_weight(w3h_words[e], w3h_scales[e], "e4m3") for e in range(HOT)])
    w2h = np.stack([unpack_weight(w2h_words[e], w2h_scales[e], "e4m3") for e in range(HOT)])
    w1c = np.stack([unpack_weight(w1c_words[e], w1c_scales[e], "e2m1") for e in range(E - HOT)])
    w3c = np.stack([unpack_weight(w3c_words[e], w3c_scales[e], "e2m1") for e in range(E - HOT)])
    w2c = np.stack([unpack_weight(w2c_words[e], w2c_scales[e], "e2m1") for e in range(E - HOT)])
    idx = unstriped(offs)
    xq = unpack_weight(x_words, x_scales, "e4m3")[:, idx]
    w1 = [*w1h, *w1c]
    w3 = [*w3h, *w3c]
    w2 = [*w2h, *w2c]
    h = gelu(by_expert(w1, xq)) * by_expert(w3, xq)
    y = by_expert(w2, mxq(h, 0, "e4m3"))
    out = y
    out_0 = out
    return (out_0,) + planes(out_0)

@@ -1,0 +1,236 @@
+from contextlib import ExitStack
+
+import concourse.mybir as mybir
+from concourse.masks import make_identity
+
+F32 = mybir.dt.float32
+BF16 = mybir.dt.bfloat16
+I32 = mybir.dt.int32
+U32 = mybir.dt.uint32
+U16 = mybir.dt.uint16
+U8 = mybir.dt.uint8
+FP8X4 = mybir.dt.float8_e4m3fn_x4
+FP4X4 = mybir.dt.float4_e2m1fn_x4
+GELU = mybir.ActivationFunctionType.Gelu_apprx_tanh
+MULT = mybir.AluOpType.mult
+
+P = 128
+WIDTH = 512
+TOKENS = 512
+EXPERTS = 6
+COLD = 5
+SLOTS = 256
+GROUP = 128
+ALL_SLOTS = EXPERTS * SLOTS
+FLOPS = 2 * 3 * WIDTH * WIDTH * ALL_SLOTS
+
+ORDER = (1, 2, 3, 4, 5, 0)
+SCALAR_ROUNDS = 7
+
+
+def load_scale_rows(nc, plane, rows):
+    rest = (slice(None),) * (len(plane.shape) - 1)
+    for r in range(4):
+        nc.sync.dma_start(
+            out=plane[(slice(r, P, 32),) + rest].bitcast(I32), in_=rows[(slice(r, 16, 4),) + rest].bitcast(I32)
+        )
+
+
+def tile_moe_hot_s_glu_gelu_kernel(
+    tc, x_words, x_scales, w1h_words, w1h_scales, w3h_words, w3h_scales, w2h_words, w2h_scales,
+    w1c_words, w1c_scales, w3c_words, w3c_scales, w2c_words, w2c_scales, offs, out_0, out_1, out_2,
+):
+    nc = tc.nc
+    with ExitStack() as ctx:
+        keep = ctx.enter_context(tc.tile_pool(name="keep", bufs=1))
+        ring = ctx.enter_context(tc.tile_pool(name="ring", bufs=2))
+        ring3 = ctx.enter_context(tc.tile_pool(name="ring3", bufs=3))
+        psum = ctx.enter_context(tc.psum_pool(name="psum", bufs=2))
+
+        offsets = keep.tile([P, ALL_SLOTS // 16], U16, name="offsets")
+        x_w = keep.tile([P, TOKENS], U32, name="x_w", align_bytes=64)
+        x_s = keep.tile([P, TOKENS], U8, name="x_s", align_bytes=64)
+        names = ("w1", "w3", "w2")
+        cold_words = {"w1": w1c_words, "w3": w3c_words, "w2": w2c_words}
+        cold_scales = {"w1": w1c_scales, "w3": w3c_scales, "w2": w2c_scales}
+        hot_words = {"w1": w1h_words, "w3": w3h_words, "w2": w2h_words}
+        hot_scales = {"w1": w1h_scales, "w3": w3h_scales, "w2": w2h_scales}
+        first_w = {m: keep.tile([P, 2 * WIDTH], U8, name=m + "_first", align_bytes=64) for m in names}
+        rest_w = {m: keep.tile([P, COLD - 1, 2 * WIDTH], U8, name=m + "_rest", align_bytes=64) for m in names}
+        hot_w = {m: keep.tile([P, 4 * WIDTH], U8, name=m + "_hot", align_bytes=64) for m in names}
+        cold_s = {m: keep.tile([P, COLD, WIDTH], U8, name=m + "_cold_s", align_bytes=64) for m in names}
+        hot_s = {m: keep.tile([P, WIDTH], U8, name=m + "_hot_s", align_bytes=64) for m in names}
+        y_codes = keep.tile([P, ALL_SLOTS], U32, name="y_codes", align_bytes=64)
+        y_scales = keep.tile([P, ALL_SLOTS], U8, name="y_scales", align_bytes=64)
+        ident = keep.tile([P, P], F32, name="ident")
+        warm_in = keep.tile([P, 1], F32, name="warm_in")
+        warm = keep.tile([P, 1], F32, name="warm")
+
+        nc.vector.memset(x_s[:].bitcast(I32), 0)
+        for m in names:
+            nc.vector.memset(cold_s[m][:].bitcast(I32), 0)
+        for m in names:
+            nc.vector.memset(hot_s[m][:].bitcast(I32), 0)
+        nc.gpsimd.memset(warm_in[:], 0.0)
+        nc.scalar.activation(warm[:], warm_in[:], GELU)
+        make_identity(nc, ident[:])
+
+        def load_first(m):
+            nc.sync.dma_start(out=first_w[m][:].bitcast(I32), in_=cold_words[m][0, 0].bitcast(I32))
+
+        def load_cold_scales(m):
+            load_scale_rows(nc, cold_s[m], cold_scales[m].rearrange("e s q n -> q (e s) n"))
+
+        nc.sync.dma_start(offsets[:], offs)
+        nc.sync.dma_start(out=x_w[:].bitcast(I32), in_=x_words[0].rearrange("p t d -> p (t d)").bitcast(I32))
+        load_scale_rows(nc, x_s, x_scales[0])
+        for m in names:
+            load_first(m)
+            load_cold_scales(m)
+        for m in names:
+            nc.sync.dma_start(
+                out=rest_w[m][:].bitcast(I32),
+                in_=cold_words[m][1:COLD].rearrange("e s p b -> p (e s) b").bitcast(I32),
+            )
+        for m in names:
+            nc.sync.dma_start(
+                out=hot_w[m][:].bitcast(I32), in_=hot_words[m][0, 0].rearrange("p n d -> p (n d)").bitcast(I32)
+            )
+            load_scale_rows(nc, hot_s[m], hot_scales[m][0, 0])
+
+        def weight(m, e):
+            if e == 0:
+                return hot_w[m][:], hot_s[m][:]
+            if e == 1:
+                return first_w[m][:], cold_s[m][:, 0, :]
+            return rest_w[m][:, e - 2, :], cold_s[m][:, e - 1, :]
+
+        def packed(e):
+            return FP8X4 if e == 0 else FP4X4
+
+        gathered = {}
+        dealt = {}
+        hidden = {}
+        quantised = {}
+        results = {}
+
+        def gather(e):
+            xg_w = ring.tile([P, SLOTS], U32, name="xg_w", align_bytes=64)
+            xg_s = ring.tile([P, SLOTS], U8, name="xg_s", align_bytes=64)
+            mine = offsets[:, e * SLOTS // 16 : (e + 1) * SLOTS // 16]
+            nc.vector.tensor_copy(xg_w[:], x_w[:].indirect(mine))
+            nc.vector.tensor_copy(xg_s[:], x_s[:].indirect(mine))
+            gathered[e] = (xg_w, xg_s)
+
+        def deal_columns(dst, src, run):
+            nc.vector.tensor_copy(
+                out=dst.rearrange("p (t c i) -> p c t i", t=4, i=run),
+                in_=src.rearrange("p (c i t) -> p c t i", t=4, i=run),
+            )
+
+        def deal(e):
+            words, scales = weight("w2", e)
+            word_dt, word_bytes = (I32, 4) if e == 0 else (U16, 2)
+            w2_w = ring.tile([P, 4 * WIDTH], U8, name="w2_w", align_bytes=64)
+            w2_s = ring.tile([P, WIDTH], U8, name="w2_s", align_bytes=64)
+            deal_columns(w2_w[:, : word_bytes * WIDTH].bitcast(word_dt), words.bitcast(word_dt), 16 // word_bytes)
+            deal_columns(w2_s[:], scales, 16)
+            dealt[e] = (w2_w, w2_s, word_bytes)
+
+        def first_layer(n):
+            e, g = ORDER[n // 2], n % 2
+            xg_w, xg_s = gathered[e]
+            cols = slice(g * GROUP, (g + 1) * GROUP)
+            sums = []
+            for m in ("w1", "w3"):
+                acc = psum.tile([P, WIDTH], F32, name="acc_" + m)
+                words, scales = weight(m, e)
+                nc.tensor.matmul_mx(
+                    out=acc[:], lhsT=xg_w[:, cols].bitcast(FP8X4), lhsT_scale=xg_s[:, cols],
+                    rhs=words.bitcast(packed(e)), rhs_scale=scales, start=True, stop=True,
+                )
+                sums.append(acc[:].rearrange("s (p u d) -> s u p d", u=2, d=2))
+            gate = ring.tile([P, 2, P, 2], F32, name="gate")
+            nc.scalar.activation(gate[:], sums[0], GELU)
+            h = ring3.tile([P, 2, P, 2], BF16, name="h")
+            nc.vector.tensor_tensor(h[:], sums[1], gate[:], MULT)
+            hidden[n] = h
+
+        def turn(n):
+            pairs = hidden[n][:].rearrange("s u p d -> s (u p d)").bitcast(F32)
+            turned = psum.tile([P, 2, GROUP], F32, name="turned")
+            for u in range(2):
+                nc.tensor.transpose(turned[:, u, :], pairs[:, u * P : (u + 1) * P], ident[:])
+            h_t = ring3.tile([P, GROUP, 2], F32, name="h_t", align_bytes=64)
+            nc.scalar.copy(h_t[:], turned[:].rearrange("p u s -> p s u"))
+            h_w = ring3.tile([P, GROUP], U32, name="h_w", align_bytes=64)
+            h_s = ring3.tile([P, GROUP], U8, name="h_s", align_bytes=64)
+            nc.vector.quantize_mx(
+                out=h_w[:].bitcast(FP8X4), scales=h_s[:], in_=h_t[:].rearrange("p s u -> p (s u)").bitcast(BF16)
+            )
+            quantised[n] = (h_w, h_s)
+
+        def second_layer(n):
+            e, g = ORDER[n // 2], n % 2
+            w2_w, w2_s, word_bytes = dealt[e]
+            h_w, h_s = quantised[n]
+            acc = psum.tile([P, 4, GROUP], F32, name="acc_y")
+            for t in range(4):
+                nc.tensor.matmul_mx(
+                    out=acc[:, t, :],
+                    lhsT=w2_w[:, t * P * word_bytes : (t + 1) * P * word_bytes].bitcast(packed(e)),
+                    lhsT_scale=w2_s[:, t * P : (t + 1) * P],
+                    rhs=h_w[:].bitcast(FP8X4), rhs_scale=h_s[:], start=True, stop=True,
+                )
+            if g == 0:
+                results[e] = ring3.tile([P, 4, SLOTS], F32, name="y")
+            y = results[e]
+            cols = slice(g * GROUP, (g + 1) * GROUP)
+            nc.scalar.copy(y[:, :, cols], acc[:])
+            y_r = ring3.tile([P, GROUP, 4], BF16, name="y_r", align_bytes=64)
+            if n < SCALAR_ROUNDS:
+                nc.scalar.copy(y_r[:], acc[:].rearrange("p t s -> p s t"))
+            else:
+                nc.vector.tensor_copy(
+                    out=y_r[:].rearrange("p (c i) t -> p c t i", i=4),
+                    in_=y[:, :, cols].rearrange("p t (c i) -> p c t i", i=4),
+                )
+            slots = slice(e * SLOTS + g * GROUP, e * SLOTS + (g + 1) * GROUP)
+            nc.vector.quantize_mx(
+                out=y_codes[:, slots].bitcast(FP8X4), scales=y_scales[:, slots],
+                in_=y_r[:].rearrange("p s t -> p (s t)"),
+            )
+
+        out_rows = out_0.rearrange("(p t) j -> p t j", t=4)
+        out_words = out_1[0].rearrange("p j d -> p (j d)").bitcast(I32)
+
+        def store(e, lo, hi):
+            slots = slice(e * SLOTS + lo, e * SLOTS + hi)
+            nc.sync.dma_start(out=out_rows[:, :, slots], in_=results[e][:, :, lo:hi])
+            nc.sync.dma_start(out=out_words[:, slots], in_=y_codes[:, slots].bitcast(I32))
+
+        groups = 2 * EXPERTS
+        gather(ORDER[0])
+        gather(ORDER[1])
+        deal(ORDER[0])
+        for step in range(groups + 2):
+            if step < groups:
+                first_layer(step)
+            if 1 <= step <= groups:
+                turn(step - 1)
+            if step >= 2:
+                n = step - 2
+                second_layer(n)
+                if n >= groups - 2:
+                    store(ORDER[n // 2], (n % 2) * GROUP, (n % 2 + 1) * GROUP)
+                elif n % 2 == 1:
+                    store(ORDER[n // 2], 0, SLOTS)
+            if step % 2 == 1 and step // 2 + 2 < EXPERTS:
+                gather(ORDER[step // 2 + 2])
+            if step % 2 == 1 and (step + 1) // 2 < EXPERTS:
+                deal(ORDER[(step + 1) // 2])
+
+        for q in range(4):
+            nc.sync.dma_start(
+                out=out_2[0, 4 * q : 4 * q + 4, :].bitcast(I32), in_=y_scales[32 * q : 32 * q + 4, :].bitcast(I32)
+            )

@@ -19,20 +19,33 @@ WIDTH = 512
 TOKENS = 512
 EXPERTS = 6
 COLD = 5
+HOT = 0
 SLOTS = 256
 GROUP = 128
+GROUPS = EXPERTS * SLOTS // GROUP
 ALL_SLOTS = EXPERTS * SLOTS
+LIST_ROWS = 16
+LINE = 16
 FLOPS = 2 * 3 * WIDTH * WIDTH * ALL_SLOTS
 
-ORDER = (1, 2, 3, 4, 5, 0)
-SCALAR_ROUNDS = 7
+ORDER = (1, 2, 3, 4, 5, HOT)
+EARLY = 2
+STACKED = 4
+MOVED = 112
+GELU_AHEAD = 4
+TURN_LAG = 2
+OUT_LAG = 7
+SCALAR_ROUNDS = 1
+BANKS_SHARED, BANKS_W3, BANKS_TURNED = 4, 3, 1
+CODE_LAG = 2
 
 
-def load_scale_rows(nc, plane, rows):
+def load_scale_rows(queues, plane, rows, first=0):
     rest = (slice(None),) * (len(plane.shape) - 1)
     for r in range(4):
-        nc.sync.dma_start(
-            out=plane[(slice(r, P, 32),) + rest].bitcast(I32), in_=rows[(slice(r, 16, 4),) + rest].bitcast(I32)
+        queues[r % len(queues)].dma_start(
+            out=plane[(slice(first + r, P, 32),) + rest].bitcast(I32),
+            in_=rows[(slice(r, 16, 4),) + rest].bitcast(I32),
         )
 
 
@@ -43,193 +56,244 @@ def tile_moe_hot_s_glu_gelu_kernel(
     nc = tc.nc
     with ExitStack() as ctx:
         keep = ctx.enter_context(tc.tile_pool(name="keep", bufs=1))
-        ring = ctx.enter_context(tc.tile_pool(name="ring", bufs=2))
-        ring3 = ctx.enter_context(tc.tile_pool(name="ring3", bufs=3))
-        psum = ctx.enter_context(tc.psum_pool(name="psum", bufs=2))
+        per_expert = ctx.enter_context(tc.tile_pool(name="per_expert", bufs=EXPERTS))
+        ring = ctx.enter_context(tc.tile_pool(name="ring", bufs=3))
+        psum = ctx.enter_context(tc.psum_pool(name="psum", bufs=1))
 
-        offsets = keep.tile([P, ALL_SLOTS // 16], U16, name="offsets")
+        matrices = ("w1", "w3", "w2")
+        first_layer = ("w1", "w3")
+        cold_words = {"w1": w1c_words, "w3": w3c_words, "w2": w2c_words}
+        cold_scales = {"w1": w1c_scales, "w3": w3c_scales}
+        hot_words = {"w1": w1h_words, "w3": w3h_words, "w2": w2h_words}
+        hot_scales = {"w1": w1h_scales, "w3": w3h_scales}
+
+        offsets = keep.tile([P, ALL_SLOTS // LIST_ROWS], U16, name="offsets")
         x_w = keep.tile([P, TOKENS], U32, name="x_w", align_bytes=64)
         x_s = keep.tile([P, TOKENS], U8, name="x_s", align_bytes=64)
-        names = ("w1", "w3", "w2")
-        cold_words = {"w1": w1c_words, "w3": w3c_words, "w2": w2c_words}
-        cold_scales = {"w1": w1c_scales, "w3": w3c_scales, "w2": w2c_scales}
-        hot_words = {"w1": w1h_words, "w3": w3h_words, "w2": w2h_words}
-        hot_scales = {"w1": w1h_scales, "w3": w3h_scales, "w2": w2h_scales}
-        first_w = {m: keep.tile([P, 2 * WIDTH], U8, name=m + "_first", align_bytes=64) for m in names}
-        rest_w = {m: keep.tile([P, COLD - 1, 2 * WIDTH], U8, name=m + "_rest", align_bytes=64) for m in names}
-        hot_w = {m: keep.tile([P, 4 * WIDTH], U8, name=m + "_hot", align_bytes=64) for m in names}
-        cold_s = {m: keep.tile([P, COLD, WIDTH], U8, name=m + "_cold_s", align_bytes=64) for m in names}
-        hot_s = {m: keep.tile([P, WIDTH], U8, name=m + "_hot_s", align_bytes=64) for m in names}
+        early_w = {m: keep.tile([P, EARLY, 2 * WIDTH], U8, name=m + "_early", align_bytes=64) for m in matrices}
+        rest_w = {m: keep.tile([P, COLD - EARLY, 2 * WIDTH], U8, name=m + "_rest", align_bytes=64) for m in matrices}
+        hot_w = {m: keep.tile([P, 4 * WIDTH], U8, name=m + "_hot", align_bytes=64) for m in matrices}
+        cold_s = {m: keep.tile([P, COLD, WIDTH], U8, name=m + "_cold_s", align_bytes=64) for m in first_layer}
+        hot_s = {m: keep.tile([P, WIDTH], U8, name=m + "_hot_s", align_bytes=64) for m in first_layer}
+        stack = [keep.tile([P, WIDTH], U8, name="stack%d" % s, align_bytes=64) for s in range(2)]
+        stack_dealt = [keep.tile([P, WIDTH], U8, name="stack_dealt%d" % s, align_bytes=64) for s in range(2)]
+        moved_down = [keep.tile([P, WIDTH], U8, name="moved_down%d" % a, align_bytes=64) for a in range(1, STACKED)]
         y_codes = keep.tile([P, ALL_SLOTS], U32, name="y_codes", align_bytes=64)
         y_scales = keep.tile([P, ALL_SLOTS], U8, name="y_scales", align_bytes=64)
         ident = keep.tile([P, P], F32, name="ident")
         warm_in = keep.tile([P, 1], F32, name="warm_in")
-        warm = keep.tile([P, 1], F32, name="warm")
+        warm_out = keep.tile([P, 1], F32, name="warm_out")
 
         nc.vector.memset(x_s[:].bitcast(I32), 0)
-        for m in names:
-            nc.vector.memset(cold_s[m][:].bitcast(I32), 0)
-        for m in names:
-            nc.vector.memset(hot_s[m][:].bitcast(I32), 0)
-        nc.gpsimd.memset(warm_in[:], 0.0)
-        nc.scalar.activation(warm[:], warm_in[:], GELU)
+        nc.vector.memset(cold_s["w1"][:].bitcast(I32), 0)
+        nc.vector.memset(warm_in[:], 0.0)
+        nc.vector.memset(cold_s["w3"][:].bitcast(I32), 0)
+        for plane in stack:
+            nc.gpsimd.memset(plane[:].bitcast(I32), 0)
         make_identity(nc, ident[:])
+        for plane in [hot_s[m] for m in first_layer] + moved_down:
+            nc.gpsimd.memset(plane[:].bitcast(I32), 0)
 
-        def load_first(m):
-            nc.sync.dma_start(out=first_w[m][:].bitcast(I32), in_=cold_words[m][0, 0].bitcast(I32))
-
-        def load_cold_scales(m):
-            load_scale_rows(nc, cold_s[m], cold_scales[m].rearrange("e s q n -> q (e s) n"))
-
-        nc.sync.dma_start(offsets[:], offs)
-        nc.sync.dma_start(out=x_w[:].bitcast(I32), in_=x_words[0].rearrange("p t d -> p (t d)").bitcast(I32))
-        load_scale_rows(nc, x_s, x_scales[0])
-        for m in names:
-            load_first(m)
-            load_cold_scales(m)
-        for m in names:
+        def load_cold_words(tile, m, lo, hi):
             nc.sync.dma_start(
-                out=rest_w[m][:].bitcast(I32),
-                in_=cold_words[m][1:COLD].rearrange("e s p b -> p (e s) b").bitcast(I32),
+                out=tile[m][:].bitcast(I32), in_=cold_words[m][lo:hi].rearrange("e s p b -> p (e s) b").bitcast(I32)
             )
-        for m in names:
+
+        def load_hot_words(m):
             nc.sync.dma_start(
                 out=hot_w[m][:].bitcast(I32), in_=hot_words[m][0, 0].rearrange("p n d -> p (n d)").bitcast(I32)
             )
-            load_scale_rows(nc, hot_s[m], hot_scales[m][0, 0])
 
-        def weight(m, e):
-            if e == 0:
-                return hot_w[m][:], hot_s[m][:]
-            if e == 1:
-                return first_w[m][:], cold_s[m][:, 0, :]
-            return rest_w[m][:, e - 2, :], cold_s[m][:, e - 1, :]
+        def load_cold_scales(queues, m):
+            load_scale_rows(queues, cold_s[m], cold_scales[m].rearrange("e s b n -> b (e s) n"))
 
-        def packed(e):
-            return FP8X4 if e == 0 else FP4X4
-
-        gathered = {}
-        dealt = {}
-        hidden = {}
-        quantised = {}
-        results = {}
-
-        def gather(e):
-            xg_w = ring.tile([P, SLOTS], U32, name="xg_w", align_bytes=64)
-            xg_s = ring.tile([P, SLOTS], U8, name="xg_s", align_bytes=64)
-            mine = offsets[:, e * SLOTS // 16 : (e + 1) * SLOTS // 16]
-            nc.vector.tensor_copy(xg_w[:], x_w[:].indirect(mine))
-            nc.vector.tensor_copy(xg_s[:], x_s[:].indirect(mine))
-            gathered[e] = (xg_w, xg_s)
-
-        def deal_columns(dst, src, run):
+        def deal(dst, src, run):
             nc.vector.tensor_copy(
                 out=dst.rearrange("p (t c i) -> p c t i", t=4, i=run),
                 in_=src.rearrange("p (c i t) -> p c t i", t=4, i=run),
             )
 
-        def deal(e):
-            words, scales = weight("w2", e)
-            word_dt, word_bytes = (I32, 4) if e == 0 else (U16, 2)
-            w2_w = ring.tile([P, 4 * WIDTH], U8, name="w2_w", align_bytes=64)
-            w2_s = ring.tile([P, WIDTH], U8, name="w2_s", align_bytes=64)
-            deal_columns(w2_w[:, : word_bytes * WIDTH].bitcast(word_dt), words.bitcast(word_dt), 16 // word_bytes)
-            deal_columns(w2_s[:], scales, 16)
-            dealt[e] = (w2_w, w2_s, word_bytes)
-
-        def first_layer(n):
-            e, g = ORDER[n // 2], n % 2
-            xg_w, xg_s = gathered[e]
-            cols = slice(g * GROUP, (g + 1) * GROUP)
-            sums = []
-            for m in ("w1", "w3"):
-                acc = psum.tile([P, WIDTH], F32, name="acc_" + m)
-                words, scales = weight(m, e)
-                nc.tensor.matmul_mx(
-                    out=acc[:], lhsT=xg_w[:, cols].bitcast(FP8X4), lhsT_scale=xg_s[:, cols],
-                    rhs=words.bitcast(packed(e)), rhs_scale=scales, start=True, stop=True,
-                )
-                sums.append(acc[:].rearrange("s (p u d) -> s u p d", u=2, d=2))
-            gate = ring.tile([P, 2, P, 2], F32, name="gate")
-            nc.scalar.activation(gate[:], sums[0], GELU)
-            h = ring3.tile([P, 2, P, 2], BF16, name="h")
-            nc.vector.tensor_tensor(h[:], sums[1], gate[:], MULT)
-            hidden[n] = h
-
-        def turn(n):
-            pairs = hidden[n][:].rearrange("s u p d -> s (u p d)").bitcast(F32)
-            turned = psum.tile([P, 2, GROUP], F32, name="turned")
-            for u in range(2):
-                nc.tensor.transpose(turned[:, u, :], pairs[:, u * P : (u + 1) * P], ident[:])
-            h_t = ring3.tile([P, GROUP, 2], F32, name="h_t", align_bytes=64)
-            nc.scalar.copy(h_t[:], turned[:].rearrange("p u s -> p s u"))
-            h_w = ring3.tile([P, GROUP], U32, name="h_w", align_bytes=64)
-            h_s = ring3.tile([P, GROUP], U8, name="h_s", align_bytes=64)
-            nc.vector.quantize_mx(
-                out=h_w[:].bitcast(FP8X4), scales=h_s[:], in_=h_t[:].rearrange("p s u -> p (s u)").bitcast(BF16)
+        scalar_first, sync_first = (nc.scalar, nc.sync), (nc.sync, nc.scalar)
+        nc.sync.dma_start(offsets[:], offs)
+        load_scale_rows(scalar_first, x_s, x_scales[0])
+        nc.sync.dma_start(out=x_w[:].bitcast(I32), in_=x_words[0].rearrange("p t d -> p (t d)").bitcast(I32))
+        load_cold_words(early_w, "w1", 0, EARLY)
+        load_cold_scales((nc.scalar, nc.scalar, nc.sync, nc.sync), "w1")
+        nc.scalar.activation(warm_out[:], warm_in[:], GELU)
+        load_cold_words(rest_w, "w1", EARLY, COLD)
+        load_hot_words("w1")
+        load_scale_rows(scalar_first, hot_s["w1"], hot_scales["w1"][0, 0])
+        load_cold_words(early_w, "w3", 0, EARLY)
+        load_cold_scales((nc.sync,), "w3")
+        for q in range(4):
+            sync_first[q % 2].dma_start(
+                out=stack[0][32 * q : 32 * q + 4 * STACKED, :].bitcast(I32),
+                in_=w2c_scales[0:STACKED, 0, 4 * q : 4 * q + 4, :].bitcast(I32),
             )
-            quantised[n] = (h_w, h_s)
-
-        def second_layer(n):
-            e, g = ORDER[n // 2], n % 2
-            w2_w, w2_s, word_bytes = dealt[e]
-            h_w, h_s = quantised[n]
-            acc = psum.tile([P, 4, GROUP], F32, name="acc_y")
-            for t in range(4):
-                nc.tensor.matmul_mx(
-                    out=acc[:, t, :],
-                    lhsT=w2_w[:, t * P * word_bytes : (t + 1) * P * word_bytes].bitcast(packed(e)),
-                    lhsT_scale=w2_s[:, t * P : (t + 1) * P],
-                    rhs=h_w[:].bitcast(FP8X4), rhs_scale=h_s[:], start=True, stop=True,
-                )
-            if g == 0:
-                results[e] = ring3.tile([P, 4, SLOTS], F32, name="y")
-            y = results[e]
-            cols = slice(g * GROUP, (g + 1) * GROUP)
-            nc.scalar.copy(y[:, :, cols], acc[:])
-            y_r = ring3.tile([P, GROUP, 4], BF16, name="y_r", align_bytes=64)
-            if n < SCALAR_ROUNDS:
-                nc.scalar.copy(y_r[:], acc[:].rearrange("p t s -> p s t"))
-            else:
-                nc.vector.tensor_copy(
-                    out=y_r[:].rearrange("p (c i) t -> p c t i", i=4),
-                    in_=y[:, :, cols].rearrange("p t (c i) -> p c t i", i=4),
-                )
-            slots = slice(e * SLOTS + g * GROUP, e * SLOTS + (g + 1) * GROUP)
-            nc.vector.quantize_mx(
-                out=y_codes[:, slots].bitcast(FP8X4), scales=y_scales[:, slots],
-                in_=y_r[:].rearrange("p s t -> p (s t)"),
+        load_cold_words(early_w, "w2", 0, EARLY)
+        load_cold_words(rest_w, "w3", EARLY, COLD)
+        load_cold_words(rest_w, "w2", EARLY, COLD)
+        deal(stack_dealt[0][:], stack[0][:], LINE)
+        for a in range(1, STACKED):
+            nc.sync.dma_start(
+                out=moved_down[a - 1][0:MOVED, :].bitcast(I32),
+                in_=stack_dealt[0][4 * a : 4 * a + MOVED, :].bitcast(I32),
             )
+        load_scale_rows(sync_first, stack[1], w2c_scales[STACKED, 0])
+        load_hot_words("w3")
+        load_scale_rows(sync_first, hot_s["w3"], hot_scales["w3"][0, 0])
+        load_hot_words("w2")
+        load_scale_rows(sync_first, stack[1], w2h_scales[0, 0], first=4)
+
+        w2_plane = {1: stack_dealt[0][:], STACKED + 1: stack_dealt[1][:], HOT: stack_dealt[1][4:P, :]}
+        for a in range(1, STACKED):
+            w2_plane[1 + a] = moved_down[a - 1][:]
+
+        def words_of(m, e):
+            if e == HOT:
+                return hot_w[m][:]
+            return early_w[m][:, e - 1, :] if e <= EARLY else rest_w[m][:, e - 1 - EARLY, :]
+
+        def plane_of(m, e):
+            return hot_s[m][:] if e == HOT else cold_s[m][:, e - 1, :]
+
+        def packed(e):
+            return FP8X4 if e == HOT else FP4X4
+
+        def word_bytes(e):
+            return 4 if e == HOT else 2
 
         out_rows = out_0.rearrange("(p t) j -> p t j", t=4)
         out_words = out_1[0].rearrange("p j d -> p (j d)").bitcast(I32)
+        gathered, gates, hidden, quantised, w2_dealt, results, rounded = {}, {}, {}, {}, {}, {}, {}
 
-        def store(e, lo, hi):
-            slots = slice(e * SLOTS + lo, e * SLOTS + hi)
-            nc.sync.dma_start(out=out_rows[:, :, slots], in_=results[e][:, :, lo:hi])
+        def gather(e):
+            xg_w = per_expert.tile([P, SLOTS], U32, name="xg_w", align_bytes=64)
+            xg_s = per_expert.tile([P, SLOTS], U8, name="xg_s", align_bytes=64)
+            mine = offsets[:, e * SLOTS // LIST_ROWS : (e + 1) * SLOTS // LIST_ROWS]
+            nc.vector.tensor_copy(xg_w[:], x_w[:].indirect(mine))
+            nc.vector.tensor_copy(xg_s[:], x_s[:].indirect(mine))
+            gathered[e] = (xg_w, xg_s)
+
+        def first_product(g, m, acc):
+            e = ORDER[g // 2]
+            xg_w, xg_s = gathered[e]
+            cols = slice(g % 2 * GROUP, (g % 2 + 1) * GROUP)
+            nc.tensor.matmul_mx(
+                out=acc[:], lhsT=xg_w[:, cols].bitcast(FP8X4), lhsT_scale=xg_s[:, cols],
+                rhs=words_of(m, e).bitcast(packed(e)), rhs_scale=plane_of(m, e), start=True, stop=True,
+            )
+            return acc[:].rearrange("s (p u d) -> s u p d", u=2, d=2)
+
+        def gelu(g):
+            acc = psum.tile([P, WIDTH], F32, name="acc_w1", tag="shared", bufs=BANKS_SHARED)
+            gate = ring.tile([P, 2, P, 2], F32, name="gate", bufs=GROUPS)
+            nc.scalar.activation(gate[:], first_product(g, "w1", acc), GELU)
+            gates[g] = gate
+
+        def gated_product(g):
+            acc = psum.tile([P, WIDTH], F32, name="acc_w3", bufs=BANKS_W3)
+            h = per_expert.tile([P, 2, P, 2], BF16, name="h")
+            nc.vector.tensor_tensor(h[:], first_product(g, "w3", acc), gates[g][:], MULT)
+            hidden[g] = h
+
+        def turn(first, count):
+            turned = psum.tile([P, 2, 2, GROUP], F32, name="turned", bufs=BANKS_TURNED)
+            for k in range(count):
+                pairs = hidden[first + k][:].rearrange("s u p d -> s (u p d)").bitcast(F32)
+                for u in range(2):
+                    nc.tensor.transpose(turned[:, k, u, :], pairs[:, u * P : (u + 1) * P], ident[:])
+            h_t = ring.tile([P, 2, GROUP, 2], F32, name="h_t", align_bytes=64)
+            nc.scalar.copy(h_t[:, :count], turned[:, :count].rearrange("p k u s -> p k s u"))
+            h_w = per_expert.tile([P, SLOTS], U32, name="h_w", align_bytes=64)
+            h_s = per_expert.tile([P, SLOTS], U8, name="h_s", align_bytes=64)
+            nc.vector.quantize_mx(
+                out=h_w[:, : count * GROUP].bitcast(FP8X4), scales=h_s[:, : count * GROUP],
+                in_=h_t[:, :count].rearrange("p k s u -> p (k s u)").bitcast(BF16),
+            )
+            for k in range(count):
+                quantised[first + k] = (h_w[:, k * GROUP : (k + 1) * GROUP], h_s[:, k * GROUP : (k + 1) * GROUP])
+
+        def deal_w2(e):
+            size = word_bytes(e)
+            word_dt = I32 if e == HOT else U16
+            w2_w = ring.tile([P, 4 * WIDTH], U8, name="w2_w", align_bytes=64)
+            deal(w2_w[:, : size * WIDTH].bitcast(word_dt), words_of("w2", e).bitcast(word_dt), LINE // size)
+            w2_dealt[e] = w2_w
+            if e == STACKED + 1:
+                deal(stack_dealt[1][:], stack[1][:], LINE)
+
+        def store_codes(e):
+            slots = slice(e * SLOTS, (e + 1) * SLOTS)
             nc.sync.dma_start(out=out_words[:, slots], in_=y_codes[:, slots].bitcast(I32))
 
-        groups = 2 * EXPERTS
-        gather(ORDER[0])
-        gather(ORDER[1])
-        deal(ORDER[0])
-        for step in range(groups + 2):
-            if step < groups:
-                first_layer(step)
-            if 1 <= step <= groups:
-                turn(step - 1)
-            if step >= 2:
-                n = step - 2
-                second_layer(n)
-                if n >= groups - 2:
-                    store(ORDER[n // 2], (n % 2) * GROUP, (n % 2 + 1) * GROUP)
-                elif n % 2 == 1:
-                    store(ORDER[n // 2], 0, SLOTS)
-            if step % 2 == 1 and step // 2 + 2 < EXPERTS:
-                gather(ORDER[step // 2 + 2])
-            if step % 2 == 1 and (step + 1) // 2 < EXPERTS:
-                deal(ORDER[(step + 1) // 2])
+        def second_layer(g):
+            place, half = divmod(g, 2)
+            e = ORDER[place]
+            size = word_bytes(e)
+            h_w, h_s = quantised[g]
+            acc = psum.tile([P, 4, GROUP], F32, name="acc_y", tag="shared", bufs=BANKS_SHARED)
+            for t in range(4):
+                nc.tensor.matmul_mx(
+                    out=acc[:, t, :],
+                    lhsT=w2_dealt[e][:, t * P * size : (t + 1) * P * size].bitcast(packed(e)),
+                    lhsT_scale=w2_plane[e][:, t * P : (t + 1) * P],
+                    rhs=h_w.bitcast(FP8X4), rhs_scale=h_s, start=True, stop=True,
+                )
+            if half == 0:
+                results[e] = per_expert.tile([P, 4, SLOTS], F32, name="y")
+                rounded[e] = per_expert.tile([P, SLOTS, 4], BF16, name="y_r", align_bytes=64)
+            cols = slice(half * GROUP, (half + 1) * GROUP)
+            if g < SCALAR_ROUNDS:
+                nc.scalar.copy(rounded[e][:, cols, :], acc[:].rearrange("p t s -> p s t"))
+            nc.scalar.copy(results[e][:, :, cols], acc[:])
+            if half == 1:
+                nc.sync.dma_start(out=out_rows[:, :, e * SLOTS : (e + 1) * SLOTS], in_=results[e][:])
+                if place >= CODE_LAG:
+                    store_codes(ORDER[place - CODE_LAG])
 
+        def quantise_y(first, count):
+            e = ORDER[first // 2]
+            lo, hi = first % 2 * GROUP, (first % 2 + count) * GROUP
+            unrounded = slice(lo + max(0, SCALAR_ROUNDS - first) * GROUP, hi)
+            nc.vector.tensor_copy(
+                out=rounded[e][:, unrounded, :].rearrange("p (c i) t -> p c t i", i=4),
+                in_=results[e][:, :, unrounded].rearrange("p t (c i) -> p c t i", i=4),
+            )
+            slots = slice(e * SLOTS + lo, e * SLOTS + hi)
+            nc.vector.quantize_mx(
+                out=y_codes[:, slots].bitcast(FP8X4), scales=y_scales[:, slots],
+                in_=rounded[e][:, lo:hi, :].rearrange("p s t -> p (s t)"),
+            )
+
+        for e in ORDER:
+            gather(e)
+        for g in range(GELU_AHEAD):
+            gelu(g)
+        last_expert = range(GROUPS - 2, GROUPS)
+        for step in range(GROUPS + OUT_LAG + 1):
+            g = step - TURN_LAG
+            if 0 <= g < GROUPS and g % 2 == 0:
+                deal_w2(ORDER[g // 2])
+            if step + GELU_AHEAD < GROUPS:
+                gelu(step + GELU_AHEAD)
+            if step < GROUPS:
+                gated_product(step)
+            if 0 <= g < 2 or g in last_expert:
+                turn(g, 1)
+            elif 0 <= g < GROUPS and g % 2 == 1:
+                turn(g - 1, 2)
+            g = step - OUT_LAG
+            if 0 <= g < GROUPS:
+                second_layer(g)
+            g = step - OUT_LAG - 1
+            if g in last_expert:
+                quantise_y(g, 1)
+            elif g >= 0 and g % 2 == 1:
+                quantise_y(g - 1, 2)
+
+        for e in ORDER[EXPERTS - CODE_LAG :]:
+            store_codes(e)
         for q in range(4):
             nc.sync.dma_start(
                 out=out_2[0, 4 * q : 4 * q + 4, :].bitcast(I32), in_=y_scales[32 * q : 32 * q + 4, :].bitcast(I32)

@@ -29,15 +29,13 @@ LINE = 16
 FLOPS = 2 * 3 * WIDTH * WIDTH * ALL_SLOTS
 
 ORDER = (1, 2, 3, 4, 5, HOT)
-EARLY = 2
+EARLY = 3
 STACKED = 4
 MOVED = 112
 GELU_AHEAD = 4
-TURN_LAG = 2
+TURN_LAG = 3
 OUT_LAG = 7
-SCALAR_ROUNDS = 1
-BANKS_SHARED, BANKS_W3, BANKS_TURNED = 4, 3, 1
-CODE_LAG = 2
+BANKS_SHARED, BANKS_W3, BANKS_TURNED = 4, 2, 2
 
 
 def load_scale_rows(queues, plane, rows, first=0):
@@ -78,6 +76,9 @@ def tile_moe_hot_s_glu_gelu_kernel(
         stack = [keep.tile([P, WIDTH], U8, name="stack%d" % s, align_bytes=64) for s in range(2)]
         stack_dealt = [keep.tile([P, WIDTH], U8, name="stack_dealt%d" % s, align_bytes=64) for s in range(2)]
         moved_down = [keep.tile([P, WIDTH], U8, name="moved_down%d" % a, align_bytes=64) for a in range(1, STACKED)]
+        early_dealt = keep.tile([P, EARLY, 2 * WIDTH], U8, name="early_dealt", align_bytes=64)
+        rest_dealt = keep.tile([P, COLD - EARLY, 2 * WIDTH], U8, name="rest_dealt", align_bytes=64)
+        hot_dealt = keep.tile([P, 4 * WIDTH], U8, name="hot_dealt", align_bytes=64)
         y_codes = keep.tile([P, ALL_SLOTS], U32, name="y_codes", align_bytes=64)
         y_scales = keep.tile([P, ALL_SLOTS], U8, name="y_scales", align_bytes=64)
         ident = keep.tile([P, P], F32, name="ident")
@@ -113,6 +114,12 @@ def tile_moe_hot_s_glu_gelu_kernel(
                 in_=src.rearrange("p (c i t) -> p c t i", t=4, i=run),
             )
 
+        def deal_cold_words(dst, src):
+            nc.vector.tensor_copy(
+                out=dst.bitcast(U16).rearrange("p e (t c i) -> p c e t i", t=4, i=LINE // 2),
+                in_=src.bitcast(U16).rearrange("p e (c i t) -> p c e t i", t=4, i=LINE // 2),
+            )
+
         scalar_first, sync_first = (nc.scalar, nc.sync), (nc.sync, nc.scalar)
         nc.sync.dma_start(offsets[:], offs)
         load_scale_rows(scalar_first, x_s, x_scales[0])
@@ -120,11 +127,9 @@ def tile_moe_hot_s_glu_gelu_kernel(
         load_cold_words(early_w, "w1", 0, EARLY)
         load_cold_scales((nc.scalar, nc.scalar, nc.sync, nc.sync), "w1")
         nc.scalar.activation(warm_out[:], warm_in[:], GELU)
-        load_cold_words(rest_w, "w1", EARLY, COLD)
-        load_hot_words("w1")
-        load_scale_rows(scalar_first, hot_s["w1"], hot_scales["w1"][0, 0])
         load_cold_words(early_w, "w3", 0, EARLY)
-        load_cold_scales((nc.sync,), "w3")
+        load_cold_scales(scalar_first, "w3")
+        load_cold_words(rest_w, "w1", EARLY, COLD)
         for q in range(4):
             sync_first[q % 2].dma_start(
                 out=stack[0][32 * q : 32 * q + 4 * STACKED, :].bitcast(I32),
@@ -139,20 +144,22 @@ def tile_moe_hot_s_glu_gelu_kernel(
                 out=moved_down[a - 1][0:MOVED, :].bitcast(I32),
                 in_=stack_dealt[0][4 * a : 4 * a + MOVED, :].bitcast(I32),
             )
-        load_scale_rows(sync_first, stack[1], w2c_scales[STACKED, 0])
+        load_scale_rows((nc.gpsimd,), hot_s["w1"], hot_scales["w1"][0, 0])
+        load_scale_rows((nc.gpsimd,), stack[1], w2c_scales[STACKED, 0])
+        load_scale_rows((nc.gpsimd,), stack[1], w2h_scales[0, 0], first=4)
+        load_hot_words("w1")
         load_hot_words("w3")
-        load_scale_rows(sync_first, hot_s["w3"], hot_scales["w3"][0, 0])
+        load_scale_rows((nc.sync,), hot_s["w3"], hot_scales["w3"][0, 0])
         load_hot_words("w2")
-        load_scale_rows(sync_first, stack[1], w2h_scales[0, 0], first=4)
 
         w2_plane = {1: stack_dealt[0][:], STACKED + 1: stack_dealt[1][:], HOT: stack_dealt[1][4:P, :]}
         for a in range(1, STACKED):
             w2_plane[1 + a] = moved_down[a - 1][:]
 
-        def words_of(m, e):
+        def expert_words(e, early, rest, hot):
             if e == HOT:
-                return hot_w[m][:]
-            return early_w[m][:, e - 1, :] if e <= EARLY else rest_w[m][:, e - 1 - EARLY, :]
+                return hot[:]
+            return early[:, e - 1, :] if e <= EARLY else rest[:, e - 1 - EARLY, :]
 
         def plane_of(m, e):
             return hot_s[m][:] if e == HOT else cold_s[m][:, e - 1, :]
@@ -160,12 +167,9 @@ def tile_moe_hot_s_glu_gelu_kernel(
         def packed(e):
             return FP8X4 if e == HOT else FP4X4
 
-        def word_bytes(e):
-            return 4 if e == HOT else 2
-
         out_rows = out_0.rearrange("(p t) j -> p t j", t=4)
         out_words = out_1[0].rearrange("p j d -> p (j d)").bitcast(I32)
-        gathered, gates, hidden, quantised, w2_dealt, results, rounded = {}, {}, {}, {}, {}, {}, {}
+        gathered, gates, hidden, quantised, results, rounded = {}, {}, {}, {}, {}, {}
 
         def gather(e):
             xg_w = per_expert.tile([P, SLOTS], U32, name="xg_w", align_bytes=64)
@@ -181,7 +185,8 @@ def tile_moe_hot_s_glu_gelu_kernel(
             cols = slice(g % 2 * GROUP, (g % 2 + 1) * GROUP)
             nc.tensor.matmul_mx(
                 out=acc[:], lhsT=xg_w[:, cols].bitcast(FP8X4), lhsT_scale=xg_s[:, cols],
-                rhs=words_of(m, e).bitcast(packed(e)), rhs_scale=plane_of(m, e), start=True, stop=True,
+                rhs=expert_words(e, early_w[m], rest_w[m], hot_w[m]).bitcast(packed(e)), rhs_scale=plane_of(m, e),
+                start=True, stop=True,
             )
             return acc[:].rearrange("s (p u d) -> s u p d", u=2, d=2)
 
@@ -215,11 +220,12 @@ def tile_moe_hot_s_glu_gelu_kernel(
                 quantised[first + k] = (h_w[:, k * GROUP : (k + 1) * GROUP], h_s[:, k * GROUP : (k + 1) * GROUP])
 
         def deal_w2(e):
-            size = word_bytes(e)
-            word_dt = I32 if e == HOT else U16
-            w2_w = ring.tile([P, 4 * WIDTH], U8, name="w2_w", align_bytes=64)
-            deal(w2_w[:, : size * WIDTH].bitcast(word_dt), words_of("w2", e).bitcast(word_dt), LINE // size)
-            w2_dealt[e] = w2_w
+            if e == 1:
+                deal_cold_words(early_dealt[:], early_w["w2"][:])
+            elif e == EARLY + 1:
+                deal_cold_words(rest_dealt[:], rest_w["w2"][:])
+            elif e == HOT:
+                deal(hot_dealt[:].bitcast(I32), hot_w["w2"][:].bitcast(I32), LINE // 4)
             if e == STACKED + 1:
                 deal(stack_dealt[1][:], stack[1][:], LINE)
 
@@ -230,35 +236,32 @@ def tile_moe_hot_s_glu_gelu_kernel(
         def second_layer(g):
             place, half = divmod(g, 2)
             e = ORDER[place]
-            size = word_bytes(e)
+            w2_words = expert_words(e, early_dealt, rest_dealt, hot_dealt)
+            block = P * (4 if e == HOT else 2)
             h_w, h_s = quantised[g]
             acc = psum.tile([P, 4, GROUP], F32, name="acc_y", tag="shared", bufs=BANKS_SHARED)
             for t in range(4):
                 nc.tensor.matmul_mx(
                     out=acc[:, t, :],
-                    lhsT=w2_dealt[e][:, t * P * size : (t + 1) * P * size].bitcast(packed(e)),
+                    lhsT=w2_words[:, t * block : (t + 1) * block].bitcast(packed(e)),
                     lhsT_scale=w2_plane[e][:, t * P : (t + 1) * P],
                     rhs=h_w.bitcast(FP8X4), rhs_scale=h_s, start=True, stop=True,
                 )
             if half == 0:
                 results[e] = per_expert.tile([P, 4, SLOTS], F32, name="y")
                 rounded[e] = per_expert.tile([P, SLOTS, 4], BF16, name="y_r", align_bytes=64)
-            cols = slice(half * GROUP, (half + 1) * GROUP)
-            if g < SCALAR_ROUNDS:
-                nc.scalar.copy(rounded[e][:, cols, :], acc[:].rearrange("p t s -> p s t"))
-            nc.scalar.copy(results[e][:, :, cols], acc[:])
+            nc.scalar.copy(results[e][:, :, half * GROUP : (half + 1) * GROUP], acc[:])
             if half == 1:
                 nc.sync.dma_start(out=out_rows[:, :, e * SLOTS : (e + 1) * SLOTS], in_=results[e][:])
-                if place >= CODE_LAG:
-                    store_codes(ORDER[place - CODE_LAG])
+                if place > 0:
+                    store_codes(ORDER[place - 1])
 
         def quantise_y(first, count):
             e = ORDER[first // 2]
             lo, hi = first % 2 * GROUP, (first % 2 + count) * GROUP
-            unrounded = slice(lo + max(0, SCALAR_ROUNDS - first) * GROUP, hi)
             nc.vector.tensor_copy(
-                out=rounded[e][:, unrounded, :].rearrange("p (c i) t -> p c t i", i=4),
-                in_=results[e][:, :, unrounded].rearrange("p t (c i) -> p c t i", i=4),
+                out=rounded[e][:, lo:hi, :].rearrange("p (c i) t -> p c t i", i=4),
+                in_=results[e][:, :, lo:hi].rearrange("p t (c i) -> p c t i", i=4),
             )
             slots = slice(e * SLOTS + lo, e * SLOTS + hi)
             nc.vector.quantize_mx(
@@ -271,29 +274,27 @@ def tile_moe_hot_s_glu_gelu_kernel(
         for g in range(GELU_AHEAD):
             gelu(g)
         last_expert = range(GROUPS - 2, GROUPS)
-        for step in range(GROUPS + OUT_LAG + 1):
+        for step in range(GROUPS + OUT_LAG):
             g = step - TURN_LAG
             if 0 <= g < GROUPS and g % 2 == 0:
                 deal_w2(ORDER[g // 2])
-            if step + GELU_AHEAD < GROUPS:
-                gelu(step + GELU_AHEAD)
-            if step < GROUPS:
-                gated_product(step)
-            if 0 <= g < 2 or g in last_expert:
+            if g in last_expert:
                 turn(g, 1)
             elif 0 <= g < GROUPS and g % 2 == 1:
                 turn(g - 1, 2)
             g = step - OUT_LAG
-            if 0 <= g < GROUPS:
+            if g >= 0:
                 second_layer(g)
-            g = step - OUT_LAG - 1
+            if step + GELU_AHEAD < GROUPS:
+                gelu(step + GELU_AHEAD)
+            if step < GROUPS:
+                gated_product(step)
             if g in last_expert:
                 quantise_y(g, 1)
             elif g >= 0 and g % 2 == 1:
                 quantise_y(g - 1, 2)
 
-        for e in ORDER[EXPERTS - CODE_LAG :]:
-            store_codes(e)
+        store_codes(ORDER[-1])
         for q in range(4):
             nc.sync.dma_start(
                 out=out_2[0, 4 * q : 4 * q + 4, :].bitcast(I32), in_=y_scales[32 * q : 32 * q + 4, :].bitcast(I32)

from contextlib import ExitStack

import concourse.mybir as mybir
from concourse.masks import make_identity

F32 = mybir.dt.float32
BF16 = mybir.dt.bfloat16
I32 = mybir.dt.int32
U32 = mybir.dt.uint32
U16 = mybir.dt.uint16
U8 = mybir.dt.uint8
FP8X4 = mybir.dt.float8_e4m3fn_x4
FP4X4 = mybir.dt.float4_e2m1fn_x4
GELU = mybir.ActivationFunctionType.Gelu_apprx_tanh
MULT = mybir.AluOpType.mult

P = 128
WIDTH = 512
TOKENS = 512
EXPERTS = 6
COLD = 5
HOT = 0
SLOTS = 256
GROUP = 128
GROUPS = EXPERTS * SLOTS // GROUP
ALL_SLOTS = EXPERTS * SLOTS
LIST_ROWS = 16
LINE = 16
FLOPS = 2 * 3 * WIDTH * WIDTH * ALL_SLOTS

ORDER = (1, 2, 3, 4, 5, HOT)
EARLY = 3
STACKED = 4
MOVED = 112
GELU_AHEAD = 4
TURN_LAG = 3
OUT_LAG = 7
BANKS_SHARED, BANKS_W3, BANKS_TURNED = 4, 2, 2


def load_scale_rows(queues, plane, rows, first=0):
    rest = (slice(None),) * (len(plane.shape) - 1)
    for r in range(4):
        queues[r % len(queues)].dma_start(
            out=plane[(slice(first + r, P, 32),) + rest].bitcast(I32),
            in_=rows[(slice(r, 16, 4),) + rest].bitcast(I32),
        )


def tile_moe_hot_s_glu_gelu_kernel(
    tc, x_words, x_scales, w1h_words, w1h_scales, w3h_words, w3h_scales, w2h_words, w2h_scales,
    w1c_words, w1c_scales, w3c_words, w3c_scales, w2c_words, w2c_scales, offs, out_0, out_1, out_2,
):
    nc = tc.nc
    with ExitStack() as ctx:
        keep = ctx.enter_context(tc.tile_pool(name="keep", bufs=1))
        per_expert = ctx.enter_context(tc.tile_pool(name="per_expert", bufs=EXPERTS))
        ring = ctx.enter_context(tc.tile_pool(name="ring", bufs=3))
        psum = ctx.enter_context(tc.psum_pool(name="psum", bufs=1))

        matrices = ("w1", "w3", "w2")
        first_layer = ("w1", "w3")
        cold_words = {"w1": w1c_words, "w3": w3c_words, "w2": w2c_words}
        cold_scales = {"w1": w1c_scales, "w3": w3c_scales}
        hot_words = {"w1": w1h_words, "w3": w3h_words, "w2": w2h_words}
        hot_scales = {"w1": w1h_scales, "w3": w3h_scales}

        offsets = keep.tile([P, ALL_SLOTS // LIST_ROWS], U16, name="offsets")
        x_w = keep.tile([P, TOKENS], U32, name="x_w", align_bytes=64)
        x_s = keep.tile([P, TOKENS], U8, name="x_s", align_bytes=64)
        early_w = {m: keep.tile([P, EARLY, 2 * WIDTH], U8, name=m + "_early", align_bytes=64) for m in matrices}
        rest_w = {m: keep.tile([P, COLD - EARLY, 2 * WIDTH], U8, name=m + "_rest", align_bytes=64) for m in matrices}
        hot_w = {m: keep.tile([P, 4 * WIDTH], U8, name=m + "_hot", align_bytes=64) for m in matrices}
        cold_s = {m: keep.tile([P, COLD, WIDTH], U8, name=m + "_cold_s", align_bytes=64) for m in first_layer}
        hot_s = {m: keep.tile([P, WIDTH], U8, name=m + "_hot_s", align_bytes=64) for m in first_layer}
        stack = [keep.tile([P, WIDTH], U8, name="stack%d" % s, align_bytes=64) for s in range(2)]
        stack_dealt = [keep.tile([P, WIDTH], U8, name="stack_dealt%d" % s, align_bytes=64) for s in range(2)]
        moved_down = [keep.tile([P, WIDTH], U8, name="moved_down%d" % a, align_bytes=64) for a in range(1, STACKED)]
        early_dealt = keep.tile([P, EARLY, 2 * WIDTH], U8, name="early_dealt", align_bytes=64)
        rest_dealt = keep.tile([P, COLD - EARLY, 2 * WIDTH], U8, name="rest_dealt", align_bytes=64)
        hot_dealt = keep.tile([P, 4 * WIDTH], U8, name="hot_dealt", align_bytes=64)
        y_codes = keep.tile([P, ALL_SLOTS], U32, name="y_codes", align_bytes=64)
        y_scales = keep.tile([P, ALL_SLOTS], U8, name="y_scales", align_bytes=64)
        ident = keep.tile([P, P], F32, name="ident")
        warm_in = keep.tile([P, 1], F32, name="warm_in")
        warm_out = keep.tile([P, 1], F32, name="warm_out")

        nc.vector.memset(x_s[:].bitcast(I32), 0)
        nc.vector.memset(cold_s["w1"][:].bitcast(I32), 0)
        nc.vector.memset(warm_in[:], 0.0)
        nc.vector.memset(cold_s["w3"][:].bitcast(I32), 0)
        for plane in stack:
            nc.gpsimd.memset(plane[:].bitcast(I32), 0)
        make_identity(nc, ident[:])
        for plane in [hot_s[m] for m in first_layer] + moved_down:
            nc.gpsimd.memset(plane[:].bitcast(I32), 0)

        def load_cold_words(tile, m, lo, hi):
            nc.sync.dma_start(
                out=tile[m][:].bitcast(I32), in_=cold_words[m][lo:hi].rearrange("e s p b -> p (e s) b").bitcast(I32)
            )

        def load_hot_words(m):
            nc.sync.dma_start(
                out=hot_w[m][:].bitcast(I32), in_=hot_words[m][0, 0].rearrange("p n d -> p (n d)").bitcast(I32)
            )

        def load_cold_scales(queues, m):
            load_scale_rows(queues, cold_s[m], cold_scales[m].rearrange("e s b n -> b (e s) n"))

        def deal(dst, src, run):
            nc.vector.tensor_copy(
                out=dst.rearrange("p (t c i) -> p c t i", t=4, i=run),
                in_=src.rearrange("p (c i t) -> p c t i", t=4, i=run),
            )

        def deal_cold_words(dst, src):
            nc.vector.tensor_copy(
                out=dst.bitcast(U16).rearrange("p e (t c i) -> p c e t i", t=4, i=LINE // 2),
                in_=src.bitcast(U16).rearrange("p e (c i t) -> p c e t i", t=4, i=LINE // 2),
            )

        scalar_first, sync_first = (nc.scalar, nc.sync), (nc.sync, nc.scalar)
        nc.sync.dma_start(offsets[:], offs)
        load_scale_rows(scalar_first, x_s, x_scales[0])
        nc.sync.dma_start(out=x_w[:].bitcast(I32), in_=x_words[0].rearrange("p t d -> p (t d)").bitcast(I32))
        load_cold_words(early_w, "w1", 0, EARLY)
        load_cold_scales((nc.scalar, nc.scalar, nc.sync, nc.sync), "w1")
        nc.scalar.activation(warm_out[:], warm_in[:], GELU)
        load_cold_words(early_w, "w3", 0, EARLY)
        load_cold_scales(scalar_first, "w3")
        load_cold_words(rest_w, "w1", EARLY, COLD)
        for q in range(4):
            sync_first[q % 2].dma_start(
                out=stack[0][32 * q : 32 * q + 4 * STACKED, :].bitcast(I32),
                in_=w2c_scales[0:STACKED, 0, 4 * q : 4 * q + 4, :].bitcast(I32),
            )
        load_cold_words(early_w, "w2", 0, EARLY)
        load_cold_words(rest_w, "w3", EARLY, COLD)
        load_cold_words(rest_w, "w2", EARLY, COLD)
        deal(stack_dealt[0][:], stack[0][:], LINE)
        for a in range(1, STACKED):
            nc.sync.dma_start(
                out=moved_down[a - 1][0:MOVED, :].bitcast(I32),
                in_=stack_dealt[0][4 * a : 4 * a + MOVED, :].bitcast(I32),
            )
        load_scale_rows((nc.gpsimd,), hot_s["w1"], hot_scales["w1"][0, 0])
        load_scale_rows((nc.gpsimd,), stack[1], w2c_scales[STACKED, 0])
        load_scale_rows((nc.gpsimd,), stack[1], w2h_scales[0, 0], first=4)
        load_hot_words("w1")
        load_hot_words("w3")
        load_scale_rows((nc.sync,), hot_s["w3"], hot_scales["w3"][0, 0])
        load_hot_words("w2")

        w2_plane = {1: stack_dealt[0][:], STACKED + 1: stack_dealt[1][:], HOT: stack_dealt[1][4:P, :]}
        for a in range(1, STACKED):
            w2_plane[1 + a] = moved_down[a - 1][:]

        def expert_words(e, early, rest, hot):
            if e == HOT:
                return hot[:]
            return early[:, e - 1, :] if e <= EARLY else rest[:, e - 1 - EARLY, :]

        def plane_of(m, e):
            return hot_s[m][:] if e == HOT else cold_s[m][:, e - 1, :]

        def packed(e):
            return FP8X4 if e == HOT else FP4X4

        out_rows = out_0.rearrange("(p t) j -> p t j", t=4)
        out_words = out_1[0].rearrange("p j d -> p (j d)").bitcast(I32)
        gathered, gates, hidden, quantised, results, rounded = {}, {}, {}, {}, {}, {}

        def gather(e):
            xg_w = per_expert.tile([P, SLOTS], U32, name="xg_w", align_bytes=64)
            xg_s = per_expert.tile([P, SLOTS], U8, name="xg_s", align_bytes=64)
            mine = offsets[:, e * SLOTS // LIST_ROWS : (e + 1) * SLOTS // LIST_ROWS]
            nc.vector.tensor_copy(xg_w[:], x_w[:].indirect(mine))
            nc.vector.tensor_copy(xg_s[:], x_s[:].indirect(mine))
            gathered[e] = (xg_w, xg_s)

        def first_product(g, m, acc):
            e = ORDER[g // 2]
            xg_w, xg_s = gathered[e]
            cols = slice(g % 2 * GROUP, (g % 2 + 1) * GROUP)
            nc.tensor.matmul_mx(
                out=acc[:], lhsT=xg_w[:, cols].bitcast(FP8X4), lhsT_scale=xg_s[:, cols],
                rhs=expert_words(e, early_w[m], rest_w[m], hot_w[m]).bitcast(packed(e)), rhs_scale=plane_of(m, e),
                start=True, stop=True,
            )
            return acc[:].rearrange("s (p u d) -> s u p d", u=2, d=2)

        def gelu(g):
            acc = psum.tile([P, WIDTH], F32, name="acc_w1", tag="shared", bufs=BANKS_SHARED)
            gate = ring.tile([P, 2, P, 2], F32, name="gate", bufs=GROUPS)
            nc.scalar.activation(gate[:], first_product(g, "w1", acc), GELU)
            gates[g] = gate

        def gated_product(g):
            acc = psum.tile([P, WIDTH], F32, name="acc_w3", bufs=BANKS_W3)
            h = per_expert.tile([P, 2, P, 2], BF16, name="h")
            nc.vector.tensor_tensor(h[:], first_product(g, "w3", acc), gates[g][:], MULT)
            hidden[g] = h

        def turn(first, count):
            turned = psum.tile([P, 2, 2, GROUP], F32, name="turned", bufs=BANKS_TURNED)
            for k in range(count):
                pairs = hidden[first + k][:].rearrange("s u p d -> s (u p d)").bitcast(F32)
                for u in range(2):
                    nc.tensor.transpose(turned[:, k, u, :], pairs[:, u * P : (u + 1) * P], ident[:])
            h_t = ring.tile([P, 2, GROUP, 2], F32, name="h_t", align_bytes=64)
            nc.scalar.copy(h_t[:, :count], turned[:, :count].rearrange("p k u s -> p k s u"))
            h_w = per_expert.tile([P, SLOTS], U32, name="h_w", align_bytes=64)
            h_s = per_expert.tile([P, SLOTS], U8, name="h_s", align_bytes=64)
            nc.vector.quantize_mx(
                out=h_w[:, : count * GROUP].bitcast(FP8X4), scales=h_s[:, : count * GROUP],
                in_=h_t[:, :count].rearrange("p k s u -> p (k s u)").bitcast(BF16),
            )
            for k in range(count):
                quantised[first + k] = (h_w[:, k * GROUP : (k + 1) * GROUP], h_s[:, k * GROUP : (k + 1) * GROUP])

        def deal_w2(e):
            if e == 1:
                deal_cold_words(early_dealt[:], early_w["w2"][:])
            elif e == EARLY + 1:
                deal_cold_words(rest_dealt[:], rest_w["w2"][:])
            elif e == HOT:
                deal(hot_dealt[:].bitcast(I32), hot_w["w2"][:].bitcast(I32), LINE // 4)
            if e == STACKED + 1:
                deal(stack_dealt[1][:], stack[1][:], LINE)

        def store_codes(e):
            slots = slice(e * SLOTS, (e + 1) * SLOTS)
            nc.sync.dma_start(out=out_words[:, slots], in_=y_codes[:, slots].bitcast(I32))

        def second_layer(g):
            place, half = divmod(g, 2)
            e = ORDER[place]
            w2_words = expert_words(e, early_dealt, rest_dealt, hot_dealt)
            block = P * (4 if e == HOT else 2)
            h_w, h_s = quantised[g]
            acc = psum.tile([P, 4, GROUP], F32, name="acc_y", tag="shared", bufs=BANKS_SHARED)
            for t in range(4):
                nc.tensor.matmul_mx(
                    out=acc[:, t, :],
                    lhsT=w2_words[:, t * block : (t + 1) * block].bitcast(packed(e)),
                    lhsT_scale=w2_plane[e][:, t * P : (t + 1) * P],
                    rhs=h_w.bitcast(FP8X4), rhs_scale=h_s, start=True, stop=True,
                )
            if half == 0:
                results[e] = per_expert.tile([P, 4, SLOTS], F32, name="y")
                rounded[e] = per_expert.tile([P, SLOTS, 4], BF16, name="y_r", align_bytes=64)
            nc.scalar.copy(results[e][:, :, half * GROUP : (half + 1) * GROUP], acc[:])
            if half == 1:
                nc.sync.dma_start(out=out_rows[:, :, e * SLOTS : (e + 1) * SLOTS], in_=results[e][:])
                if place > 0:
                    store_codes(ORDER[place - 1])

        def quantise_y(first, count):
            e = ORDER[first // 2]
            lo, hi = first % 2 * GROUP, (first % 2 + count) * GROUP
            nc.vector.tensor_copy(
                out=rounded[e][:, lo:hi, :].rearrange("p (c i) t -> p c t i", i=4),
                in_=results[e][:, :, lo:hi].rearrange("p t (c i) -> p c t i", i=4),
            )
            slots = slice(e * SLOTS + lo, e * SLOTS + hi)
            nc.vector.quantize_mx(
                out=y_codes[:, slots].bitcast(FP8X4), scales=y_scales[:, slots],
                in_=rounded[e][:, lo:hi, :].rearrange("p s t -> p (s t)"),
            )

        for e in ORDER:
            gather(e)
        for g in range(GELU_AHEAD):
            gelu(g)
        last_expert = range(GROUPS - 2, GROUPS)
        for step in range(GROUPS + OUT_LAG):
            g = step - TURN_LAG
            if 0 <= g < GROUPS and g % 2 == 0:
                deal_w2(ORDER[g // 2])
            if g in last_expert:
                turn(g, 1)
            elif 0 <= g < GROUPS and g % 2 == 1:
                turn(g - 1, 2)
            g = step - OUT_LAG
            if g >= 0:
                second_layer(g)
            if step + GELU_AHEAD < GROUPS:
                gelu(step + GELU_AHEAD)
            if step < GROUPS:
                gated_product(step)
            if g in last_expert:
                quantise_y(g, 1)
            elif g >= 0 and g % 2 == 1:
                quantise_y(g - 1, 2)

        store_codes(ORDER[-1])
        for q in range(4):
            nc.sync.dma_start(
                out=out_2[0, 4 * q : 4 * q + 4, :].bitcast(I32), in_=y_scales[32 * q : 32 * q + 4, :].bitcast(I32)
            )
